import numpy as np
import ml_dtypes


def mxq(x, axis, fmt="e4m3"):
    dtype, down = {"e4m3": (ml_dtypes.float8_e4m3fn, 7), "e5m2": (ml_dtypes.float8_e5m2, 14)}[fmt]
    v = np.moveaxis(np.asarray(x, np.float32).astype(ml_dtypes.bfloat16).astype(np.float64), axis, -1)
    blocks = v.reshape(v.shape[:-1] + (-1, 32))
    amax = np.abs(blocks).max(-1, keepdims=True)
    byte = np.maximum(np.where(amax > 0, np.frexp(amax)[1] - 1 + 127, 0) - down, 1)
    scale = np.exp2(byte - 127.0)
    codes = (blocks / scale).astype(np.float32).astype(dtype).astype(np.float64)
    return np.moveaxis((codes * scale).reshape(v.shape), -1, axis)


WIDE = False


def mx_kscale(k):
    if not WIDE:
        return np.ones(k)
    levels = np.array([10, -10, 5, -5, 0])
    if k % 512:
        return np.exp2(np.random.permutation(np.resize(levels, k // 32))).repeat(32)
    a = np.empty((k // 512, 16))
    for p in range(k // 512):
        a[p, :8] = np.random.permutation(np.resize(levels, 8))
        for g in range(8):
            far = levels[np.abs(levels - a[p, g]) >= 10]
            a[p, g + 8] = far[np.random.randint(len(far))]
    return np.exp2(a.ravel()).repeat(32)


def f64(x):
    return np.asarray(x).astype(np.float64)


def striped(idx):
    return np.tile(idx.reshape(-1, 16).T, (8, 1)).astype(np.uint16)


def unstriped(offs):
    return offs[:16].T.reshape(-1).astype(np.int64)


def striped8(idx):
    return np.concatenate([x.reshape(-1, 16).T for x in idx]).astype(np.uint16)


def runs(offs, k):
    lists = np.stack([offs[16 * r : 16 * r + 16].T.reshape(-1) for r in range(8)]).astype(np.int64)
    return lists[np.arange(k) % 512 // 64]


def pack_weight(w):
    k, n = w.shape
    w = f64(np.asarray(w, np.float32).astype(ml_dtypes.bfloat16)).reshape(k // 32, 32, n)
    amax = np.abs(w).max(1)
    byte = np.clip(np.where(amax > 0, np.frexp(amax)[1] - 1 + 127 - 7, 1), 1, 254)
    scaled = (w * np.exp2(127.0 - byte)[:, None, :]).reshape(k, n).astype(np.float32)
    words = np.ascontiguousarray(scaled.reshape(k // 512, 128, 4, n).transpose(0, 1, 3, 2)).astype(ml_dtypes.float8_e4m3fn).view(np.uint8)
    return words, np.ascontiguousarray(byte.astype(np.uint8).reshape(k // 512, 16, n))


def unpack_weight(words, scales):
    g, p, n, _ = words.shape
    vals = np.ascontiguousarray(words).view(ml_dtypes.float8_e4m3fn).astype(np.float64) * np.repeat(np.exp2(scales.astype(np.float64) - 127.0), 8, axis=1)[..., None]
    return vals.transpose(0, 1, 3, 2).reshape(g * 512, n)

def planes(y):
    n, m = y.shape
    v = y.astype(np.float32).astype(ml_dtypes.bfloat16).astype(np.float64).reshape(n // 32, 32, m)
    top = np.abs(v).max(1)
    byte = np.clip(np.where(top > 0, np.frexp(top)[1] - 1 + 127 - 7, 1), 1, 254)
    codes = (v * np.exp2(127.0 - byte)[:, None, :]).reshape(n, m).astype(np.float32).astype(ml_dtypes.float8_e4m3fn).view(np.uint8)
    words = codes.reshape(n // 512, 128, 4, m).transpose(0, 1, 3, 2)
    return np.ascontiguousarray(words), np.ascontiguousarray(byte.astype(np.uint8).reshape(n // 512, 16, m))


K, T, S, G, H, C = 512, 1024, 256, 2048, 512, 512


def setup_inputs():
    n = np.random.standard_normal
    s = mx_kscale(K)[:, None]
    packed_xT = pack_weight(n((K, T)) * s)
    packed_dT = pack_weight(n((K, G)) / s)
    return {
        "x_words": packed_xT[0],
        "x_scales": packed_xT[1],
        "d_words": packed_dT[0],
        "d_scales": packed_dT[1],
        "gs": (np.random.uniform(0.5, 1.5, (K, 1)) / s).astype(np.float32),
        "offs": striped(np.random.permutation(T)[:S]),
        "k1": striped8(np.random.randint(0, G, (8, H))),
        "n1": striped(np.random.permutation(S)),
        "n2": striped(np.random.permutation(S)),
        "cand": striped(np.random.permutation(T)[:C]),
        "n3": striped(np.random.permutation(S)),
        "n4": striped(np.random.permutation(S)),
    }


def reference(x_words, x_scales, d_words, d_scales, gs, offs, k1, n1, n2, cand, n3, n4):
    x_cand = unpack_weight(x_words, x_scales)[:, unstriped(cand)]
    d_k1 = unpack_weight(d_words, d_scales)[np.arange(K)[:, None], runs(k1, K)]
    xq = unpack_weight(x_words, x_scales)[:, unstriped(offs)]
    h = 0.0625 * (d_k1.T @ xq)
    z = f64(gs) * (np.maximum(h[:, unstriped(n1)], h[:, unstriped(n2)]) - (0.75 * h))
    s = 0.0625 * ((x_cand.T @ mxq(z, 0, "e4m3")))
    pa = s[:, unstriped(n3)]
    pb = s[:, unstriped(n4)]
    out_0 = np.maximum(np.maximum(s, pa), pb) - (0.5 * (np.minimum(np.minimum(s, pa), pb)))
    return (out_0,) + planes(out_0)

@@ -1,0 +1,168 @@
+from contextlib import ExitStack
+
+import concourse.mybir as mybir
+
+F32 = mybir.dt.float32
+BF16 = mybir.dt.bfloat16
+I32 = mybir.dt.int32
+U32 = mybir.dt.uint32
+U16 = mybir.dt.uint16
+U8 = mybir.dt.uint8
+FP8X4 = mybir.dt.float8_e4m3fn_x4
+ALU = mybir.AluOpType
+COPY = mybir.ActivationFunctionType.Copy
+
+P = 128
+K, T, S, G, H, C = 512, 1024, 256, 2048, 512, 512
+HALF = S // 2
+FLOPS = 2 * K * H * S + 2 * K * C * S
+
+
+def tile_picked_pqcoverrange_none_po_kernel(tc, x_words, x_scales, d_words, d_scales, gs, offs, k1, n1, n2, cand, n3, n4, out_0, out_1, out_2):
+    nc = tc.nc
+    with ExitStack() as ctx:
+        sb = ctx.enter_context(tc.tile_pool(name="sb", bufs=1))
+        late = ctx.enter_context(tc.tile_pool(name="late", bufs=1))
+        ps = ctx.enter_context(tc.psum_pool(name="ps", bufs=1))
+
+        def tile(shape, dtype, name):
+            return sb.tile(shape, dtype, name=name, align_bytes=64)
+
+        def load_list(src, name):
+            t = tile(list(src.shape), U16, name)
+            nc.sync.dma_start(out=t[:], in_=src)
+            return t
+
+        ds_tab = tile([P, G], U8, "ds_tab")
+        xs_tab = tile([P, T], U8, "xs_tab")
+        ds_mm = tile([P, H], U8, "ds_mm")
+        nc.vector.memset(ds_tab[:].bitcast(U32), 0)
+        nc.vector.memset(xs_tab[:].bitcast(U32), 0)
+        nc.vector.memset(ds_mm[:].bitcast(U32), 0)
+        k1_t = load_list(k1, "k1_t")
+        offs_t = load_list(offs, "offs_t")
+        nc.sync.dma_start(out=ds_tab[0:P:8, :].bitcast(I32), in_=d_scales[0].bitcast(I32))
+        dw_tab = tile([P, G], U32, "dw_tab")
+        nc.sync.dma_start(out=dw_tab[:].bitcast(I32), in_=d_words[0].rearrange("p n t -> p (n t)").bitcast(I32))
+        xw_tab = tile([P, T], U32, "xw_tab")
+        nc.sync.dma_start(out=xw_tab[:].bitcast(I32), in_=x_words[0].rearrange("p n t -> p (n t)").bitcast(I32))
+        for q in range(4):
+            nc.scalar.dma_start(out=xs_tab[32 * q : 32 * q + 4, :].bitcast(I32), in_=x_scales[0, 4 * q : 4 * q + 4, :].bitcast(I32))
+        cand_t = load_list(cand, "cand_t")
+        n1_t = load_list(n1, "n1_t")
+        n2_t = load_list(n2, "n2_t")
+        gs_t = tile([P, 4], F32, "gs_t")
+        nc.sync.dma_start(out=gs_t[:], in_=gs.rearrange("(p t) o -> p (t o)", t=4))
+        n3_t = load_list(n3, "n3_t")
+        n4_t = load_list(n4, "n4_t")
+
+        ds_g = tile([P, H], U8, "ds_g")
+        nc.vector.tensor_copy(out=ds_g[:], in_=ds_tab[:].indirect(k1_t[:]))
+        ds_d = tile([P, H], U8, "ds_d")
+        nc.vector.tensor_copy(out=ds_d[:].rearrange("p (t m) -> p m t", t=4), in_=ds_g[:].rearrange("p (m t) -> p m t", t=4))
+        for q in range(4):
+            nc.scalar.dma_start(out=ds_mm[32 * q : 32 * q + 4, :].bitcast(I32), in_=ds_d[32 * q : 32 * q + 32 : 8, :].bitcast(I32))
+        xs_o = tile([P, S], U8, "xs_o")
+        nc.vector.tensor_copy(out=xs_o[:], in_=xs_tab[:].indirect(offs_t[:]))
+        dw_g = late.tile([P, H], U32, name="dw_g", offset=0, align_bytes=64)
+        nc.vector.tensor_copy(out=dw_g[:], in_=dw_tab[:].indirect(k1_t[:]))
+        dw_d = tile([P, H], U32, "dw_d")
+        nc.vector.tensor_copy(out=dw_d[:].rearrange("p (t m) -> p m t", t=4), in_=dw_g[:].rearrange("p (m t) -> p m t", t=4))
+        xw_o = tile([P, S], U32, "xw_o")
+        nc.vector.tensor_copy(out=xw_o[:], in_=xw_tab[:].indirect(offs_t[:]))
+
+        h = tile([P, 4, S], F32, "h")
+        for t in range(4):
+            acc = ps.tile([P, S], F32, name="acc", tag="bank%d" % t)
+            cols = slice(P * t, P * (t + 1))
+            nc.tensor.matmul_mx(out=acc[:], lhsT=dw_d[:, cols].bitcast(FP8X4), lhsT_scale=ds_mm[:, cols],
+                                rhs=xw_o[:].bitcast(FP8X4), rhs_scale=xs_o[:], start=True, stop=True)
+            nc.scalar.activation(out=h[:, t, :], in_=acc[:], func=COPY, scale=0.0625)
+
+        xw_c = late.tile([P, C], U32, name="xw_c", offset=C, align_bytes=64)
+        xs_c = late.tile([P, C], U8, name="xs_c", offset=0, align_bytes=64)
+        nc.vector.tensor_copy(out=xs_c[:].rearrange("p (t m) -> p m t", t=4), in_=xs_tab[:].indirect(cand_t[:]))
+        nc.vector.tensor_copy(out=xw_c[:].rearrange("p (t m) -> p m t", t=4), in_=xw_tab[:].indirect(cand_t[:]))
+
+        s = tile([P, 4, S], F32, "s")
+        for hf in range(2):
+            cols = slice(HALF * hf, HALF * (hf + 1))
+            lcols = slice(8 * hf, 8 * hf + 8)
+            g1 = tile([P, 4, HALF], F32, "g1_%d" % hf)
+            g2 = tile([P, 4, HALF], F32, "g2_%d" % hf)
+            mx = tile([P, 4, HALF], F32, "mx_%d" % hf)
+            u = tile([P, 4, HALF], F32, "u_%d" % hf)
+            for t in range(4):
+                nc.scalar.activation(out=g1[:, t, :], in_=h[:, t, :].indirect(n1_t[:, lcols]), func=COPY)
+                if hf == 0:
+                    nc.vector.tensor_copy(out=g2[:, t, :], in_=h[:, t, :].indirect(n2_t[:, lcols]))
+                else:
+                    nc.scalar.activation(out=g2[:, t, :], in_=h[:, t, :].indirect(n2_t[:, lcols]), func=COPY)
+            for tp in range(2):
+                ts = slice(2 * tp, 2 * tp + 2)
+                nc.vector.tensor_tensor(out=mx[:, ts, :], in0=g1[:, ts, :], in1=g2[:, ts, :], op=ALU.max)
+                nc.vector.scalar_tensor_tensor(out=u[:, ts, :], in0=h[:, ts, cols], scalar=-0.75, in1=mx[:, ts, :], op0=ALU.mult, op1=ALU.add)
+            zb = tile([P, HALF, 4], BF16, "zb_%d" % hf)
+            nc.vector.tensor_tensor(out=zb[:].rearrange("p (c i) t -> p c t i", i=4), in0=u[:].rearrange("p t (c i) -> p c t i", i=4),
+                                    in1=gs_t[:].unsqueeze(1).unsqueeze(3).to_broadcast([P, HALF // 4, 4, 4]), op=ALU.mult)
+            zw = tile([P, HALF], U32, "zw_%d" % hf)
+            zs = tile([P, HALF], U8, "zs_%d" % hf)
+            nc.vector.quantize_mx(out=zw[:].bitcast(FP8X4), scales=zs[:], in_=zb[:].rearrange("p c t -> p (c t)"))
+            if hf == 0:
+                acc0 = ps.tile([P, 4, HALF], F32, name="acc0", tag="bank4")
+            for t in range(4):
+                ccols = slice(P * t, P * (t + 1))
+                if hf == 0:
+                    dst = acc0[:, t, :]
+                else:
+                    acc1 = ps.tile([P, HALF], F32, name="acc1", tag="bank%d" % t)
+                    dst = acc1[:]
+                nc.tensor.matmul_mx(out=dst, lhsT=xw_c[:, ccols].bitcast(FP8X4), lhsT_scale=xs_c[:, ccols],
+                                    rhs=zw[:].bitcast(FP8X4), rhs_scale=zs[:], start=True, stop=True)
+                if hf == 1:
+                    if t == 0:
+                        nc.scalar.activation(out=s[:, t, cols], in_=dst, func=COPY, scale=0.0625)
+                    else:
+                        nc.vector.tensor_scalar(out=s[:, t, cols], in0=dst, scalar1=0.0625, scalar2=None, op0=ALU.mult)
+            if hf == 0:
+                nc.scalar.activation(out=s[:, :, cols], in_=acc0[:], func=COPY, scale=0.0625)
+
+        ow = tile([P, S], U32, "ow")
+        osc = tile([P, S], U8, "osc")
+        out_rows = out_0.rearrange("(p t) c -> p t c", t=4)
+        out_words = out_1[0].rearrange("p n t -> p (n t)").bitcast(I32)
+        for hf in range(2):
+            cols = slice(HALF * hf, HALF * (hf + 1))
+            lcols = slice(8 * hf, 8 * hf + 8)
+            pa = tile([P, 4, HALF], F32, "pa_%d" % hf)
+            pb = tile([P, 4, HALF], F32, "pb_%d" % hf)
+            hi = tile([P, 4, HALF], F32, "hi_%d" % hf)
+            lo = tile([P, 4, HALF], F32, "lo_%d" % hf)
+            hi2 = tile([P, 4, HALF], F32, "hi2_%d" % hf)
+            lo2 = tile([P, 4, HALF], F32, "lo2_%d" % hf)
+            y = tile([P, 4, HALF], F32, "y_%d" % hf)
+            for t in range(4):
+                nc.scalar.activation(out=pa[:, t, :], in_=s[:, t, :].indirect(n3_t[:, lcols]), func=COPY)
+                nc.scalar.activation(out=pb[:, t, :], in_=s[:, t, :].indirect(n4_t[:, lcols]), func=COPY)
+            groups = [slice(0, 1), slice(1, 2), slice(2, 4)] if hf == 0 else [slice(0, 2), slice(2, 4)]
+            for ts in groups:
+                nc.vector.tensor_tensor(out=hi[:, ts, :], in0=pa[:, ts, :], in1=s[:, ts, cols], op=ALU.max)
+                nc.vector.tensor_tensor(out=lo[:, ts, :], in0=pa[:, ts, :], in1=s[:, ts, cols], op=ALU.min)
+                nc.vector.tensor_tensor(out=hi2[:, ts, :], in0=hi[:, ts, :], in1=pb[:, ts, :], op=ALU.max)
+                nc.vector.tensor_tensor(out=lo2[:, ts, :], in0=lo[:, ts, :], in1=pb[:, ts, :], op=ALU.min)
+                nc.vector.scalar_tensor_tensor(out=y[:, ts, :], in0=lo2[:, ts, :], scalar=-0.5, in1=hi2[:, ts, :], op0=ALU.mult, op1=ALU.add)
+                if ts.stop == 4 or hf == 1:
+                    st = ts if hf == 1 else slice(0, 4)
+                    nc.sync.dma_start(out=out_rows[:, st, cols], in_=y[:, st, :])
+            yb = tile([P, HALF, 4], BF16, "yb_%d" % hf)
+            yb_v = yb[:].rearrange("p (c i) t -> p c t i", i=4)
+            y_v = y[:].rearrange("p t (c i) -> p c t i", i=4)
+            if hf == 0:
+                nc.scalar.copy(out=yb_v, in_=y_v)
+            else:
+                nc.vector.tensor_copy(out=yb_v, in_=y_v)
+            nc.vector.quantize_mx(out=ow[:, cols].bitcast(FP8X4), scales=osc[:, cols], in_=yb[:].rearrange("p c t -> p (c t)"))
+            nc.scalar.dma_start(out=out_words[:, cols], in_=ow[:, cols].bitcast(I32))
+        for q in range(4):
+            eng = nc.sync if q % 2 == 0 else nc.scalar
+            eng.dma_start(out=out_2[0, 4 * q : 4 * q + 4, :].bitcast(I32), in_=osc[32 * q : 32 * q + 4, :].bitcast(I32))

@@ -35,134 +35,146 @@ def tile_picked_pqcoverrange_none_po_kernel(tc, x_words, x_scales, d_words, d_sc
 
         ds_tab = tile([P, G], U8, "ds_tab")
         xs_tab = tile([P, T], U8, "xs_tab")
-        ds_mm = tile([P, H], U8, "ds_mm")
-        nc.vector.memset(ds_tab[:].bitcast(U32), 0)
-        nc.vector.memset(xs_tab[:].bitcast(U32), 0)
-        nc.vector.memset(ds_mm[:].bitcast(U32), 0)
+        nc.gpsimd.memset(xs_tab[:].bitcast(U32), 0)
         k1_t = load_list(k1, "k1_t")
-        offs_t = load_list(offs, "offs_t")
-        nc.sync.dma_start(out=ds_tab[0:P:8, :].bitcast(I32), in_=d_scales[0].bitcast(I32))
+        ds_rows = d_scales[0].bitcast(I32)
+        for e in range(2):
+            nc.sync.dma_start(out=ds_tab[e:P:2, :].bitcast(I32), in_=ds_rows[e:16:2, :].unsqueeze(1).to_broadcast([8, 8, G // 4]))
         dw_tab = tile([P, G], U32, "dw_tab")
         nc.sync.dma_start(out=dw_tab[:].bitcast(I32), in_=d_words[0].rearrange("p n t -> p (n t)").bitcast(I32))
-        xw_tab = tile([P, T], U32, "xw_tab")
-        nc.sync.dma_start(out=xw_tab[:].bitcast(I32), in_=x_words[0].rearrange("p n t -> p (n t)").bitcast(I32))
         for q in range(4):
             nc.scalar.dma_start(out=xs_tab[32 * q : 32 * q + 4, :].bitcast(I32), in_=x_scales[0, 4 * q : 4 * q + 4, :].bitcast(I32))
+        offs_t = load_list(offs, "offs_t")
+        xw_tab = tile([P, T], U32, "xw_tab")
+        nc.sync.dma_start(out=xw_tab[:].bitcast(I32), in_=x_words[0].rearrange("p n t -> p (n t)").bitcast(I32))
         cand_t = load_list(cand, "cand_t")
         n1_t = load_list(n1, "n1_t")
         n2_t = load_list(n2, "n2_t")
-        gs_t = tile([P, 4], F32, "gs_t")
-        nc.sync.dma_start(out=gs_t[:], in_=gs.rearrange("(p t) o -> p (t o)", t=4))
         n3_t = load_list(n3, "n3_t")
         n4_t = load_list(n4, "n4_t")
 
-        ds_g = tile([P, H], U8, "ds_g")
+        ds_g = late.tile([P, H], U8, name="ds_g", align_bytes=64, offset=4096)
         nc.vector.tensor_copy(out=ds_g[:], in_=ds_tab[:].indirect(k1_t[:]))
-        ds_d = tile([P, H], U8, "ds_d")
-        nc.vector.tensor_copy(out=ds_d[:].rearrange("p (t m) -> p m t", t=4), in_=ds_g[:].rearrange("p (m t) -> p m t", t=4))
-        for q in range(4):
-            nc.scalar.dma_start(out=ds_mm[32 * q : 32 * q + 4, :].bitcast(I32), in_=ds_d[32 * q : 32 * q + 32 : 8, :].bitcast(I32))
-        xs_o = tile([P, S], U8, "xs_o")
+        ds_mm = tile([P, H], U8, "ds_mm")
+        nc.vector.tensor_copy(out=ds_mm[:].rearrange("p (t m) -> p m t", t=4), in_=ds_g[:].rearrange("p (m t) -> p m t", t=4))
+        for e in range(2):
+            nc.scalar.dma_start(out=ds_mm[2 + e : P : 32, :].bitcast(I32), in_=ds_mm[16 + e : P : 32, :].bitcast(I32))
+        xs_o = late.tile([P, S], U8, name="xs_o", offset=4096, align_bytes=64)
         nc.vector.tensor_copy(out=xs_o[:], in_=xs_tab[:].indirect(offs_t[:]))
         dw_g = late.tile([P, H], U32, name="dw_g", offset=0, align_bytes=64)
         nc.vector.tensor_copy(out=dw_g[:], in_=dw_tab[:].indirect(k1_t[:]))
         dw_d = tile([P, H], U32, "dw_d")
         nc.vector.tensor_copy(out=dw_d[:].rearrange("p (t m) -> p m t", t=4), in_=dw_g[:].rearrange("p (m t) -> p m t", t=4))
-        xw_o = tile([P, S], U32, "xw_o")
+        xw_o = late.tile([P, S], U32, name="xw_o", offset=64 + C, align_bytes=64)
         nc.vector.tensor_copy(out=xw_o[:], in_=xw_tab[:].indirect(offs_t[:]))
+        gs_t = late.tile([P, 4], F32, name="gs_t", align_bytes=64, offset=0)
+        nc.sync.dma_start(out=gs_t[:], in_=gs.rearrange("(p t) o -> p (t o)", t=4))
 
-        h = tile([P, 4, S], F32, "h")
+        h = tile([P, 4 * S], F32, "h")
         for t in range(4):
-            acc = ps.tile([P, S], F32, name="acc", tag="bank%d" % t)
+            acc = ps.tile([P, S], F32, name="acc", tag="h%d" % t)
             cols = slice(P * t, P * (t + 1))
             nc.tensor.matmul_mx(out=acc[:], lhsT=dw_d[:, cols].bitcast(FP8X4), lhsT_scale=ds_mm[:, cols],
                                 rhs=xw_o[:].bitcast(FP8X4), rhs_scale=xs_o[:], start=True, stop=True)
-            nc.scalar.activation(out=h[:, t, :], in_=acc[:], func=COPY, scale=0.0625)
+            nc.scalar.activation(out=h[:, S * t : S * (t + 1)], in_=acc[:], func=COPY, scale=0.0625)
 
-        xw_c = late.tile([P, C], U32, name="xw_c", offset=C, align_bytes=64)
-        xs_c = late.tile([P, C], U8, name="xs_c", offset=0, align_bytes=64)
+        xw_c = late.tile([P, C], U32, name="xw_c", offset=64 + C + 4 * S, align_bytes=64)
+        xs_c = late.tile([P, C], U8, name="xs_c", offset=64, align_bytes=64)
         nc.vector.tensor_copy(out=xs_c[:].rearrange("p (t m) -> p m t", t=4), in_=xs_tab[:].indirect(cand_t[:]))
         nc.vector.tensor_copy(out=xw_c[:].rearrange("p (t m) -> p m t", t=4), in_=xw_tab[:].indirect(cand_t[:]))
 
-        s = tile([P, 4, S], F32, "s")
-        for hf in range(2):
-            cols = slice(HALF * hf, HALF * (hf + 1))
-            lcols = slice(8 * hf, 8 * hf + 8)
-            g1 = tile([P, 4, HALF], F32, "g1_%d" % hf)
-            g2 = tile([P, 4, HALF], F32, "g2_%d" % hf)
-            mx = tile([P, 4, HALF], F32, "mx_%d" % hf)
-            u = tile([P, 4, HALF], F32, "u_%d" % hf)
-            for t in range(4):
-                nc.scalar.activation(out=g1[:, t, :], in_=h[:, t, :].indirect(n1_t[:, lcols]), func=COPY)
-                if hf == 0:
-                    nc.vector.tensor_copy(out=g2[:, t, :], in_=h[:, t, :].indirect(n2_t[:, lcols]))
-                else:
-                    nc.scalar.activation(out=g2[:, t, :], in_=h[:, t, :].indirect(n2_t[:, lcols]), func=COPY)
-            for tp in range(2):
-                ts = slice(2 * tp, 2 * tp + 2)
-                nc.vector.tensor_tensor(out=mx[:, ts, :], in0=g1[:, ts, :], in1=g2[:, ts, :], op=ALU.max)
-                nc.vector.scalar_tensor_tensor(out=u[:, ts, :], in0=h[:, ts, cols], scalar=-0.75, in1=mx[:, ts, :], op0=ALU.mult, op1=ALU.add)
-            zb = tile([P, HALF, 4], BF16, "zb_%d" % hf)
-            nc.vector.tensor_tensor(out=zb[:].rearrange("p (c i) t -> p c t i", i=4), in0=u[:].rearrange("p t (c i) -> p c t i", i=4),
+        pieces = [(0, 0, S), (1, 0, S), (2, 0, S), (3, 0, HALF), (3, HALF, S)]
+
+        def fetch(on_vector, dst, src, lst, t, a, b, scale=1.0):
+            width = 2 * S if b - a == S else S
+            window = src[:, S * t : S * t + width].indirect(lst[:, a // 16 : b // 16])
+            if on_vector:
+                nc.vector.tensor_copy(out=dst[:, t, a:b], in_=window)
+            else:
+                nc.scalar.activation(out=dst[:, t, a:b], in_=window, func=COPY, scale=scale)
+
+        g1 = tile([P, 4, S], F32, "g1")
+        g2 = tile([P, 4, S], F32, "g2")
+        mx = tile([P, 4, S], F32, "mx")
+        u = tile([P, 4, S], F32, "u")
+        s = tile([P, 4 * S], F32, "s")
+        s_acc = [ps.tile([P, S], F32, name="s_acc", tag="s%d" % t) for t in range(4)]
+        def larger(t, a, b):
+            fetch(False, g1, h, n1_t, t, a, b)
+            fetch(t in (0, 1), g2, h, n2_t, t, a, b)
+            nc.vector.tensor_tensor(out=mx[:, t, a:b], in0=g1[:, t, a:b], in1=g2[:, t, a:b], op=ALU.max)
+
+        def less_h(t, a, b):
+            nc.vector.scalar_tensor_tensor(out=u[:, t, a:b], in0=h[:, S * t + a : S * t + b], scalar=-0.75, in1=mx[:, t, a:b], op0=ALU.mult, op1=ALU.add)
+
+        def weigh(a, b):
+            zb = tile([P, HALF, 4], BF16, "zb_%d" % a)
+            nc.vector.tensor_tensor(out=zb[:].rearrange("p (c i) t -> p c t i", i=4), in0=u[:, :, a:b].rearrange("p t (c i) -> p c t i", i=4),
                                     in1=gs_t[:].unsqueeze(1).unsqueeze(3).to_broadcast([P, HALF // 4, 4, 4]), op=ALU.mult)
-            zw = tile([P, HALF], U32, "zw_%d" % hf)
-            zs = tile([P, HALF], U8, "zs_%d" % hf)
+            return zb
+
+        def quantise(zb, a):
+            zw = tile([P, HALF], U32, "zw_%d" % a)
+            zs = tile([P, HALF], U8, "zs_%d" % a)
             nc.vector.quantize_mx(out=zw[:].bitcast(FP8X4), scales=zs[:], in_=zb[:].rearrange("p c t -> p (c t)"))
-            if hf == 0:
-                acc0 = ps.tile([P, 4, HALF], F32, name="acc0", tag="bank4")
-            for t in range(4):
-                ccols = slice(P * t, P * (t + 1))
-                if hf == 0:
-                    dst = acc0[:, t, :]
-                else:
-                    acc1 = ps.tile([P, HALF], F32, name="acc1", tag="bank%d" % t)
-                    dst = acc1[:]
-                nc.tensor.matmul_mx(out=dst, lhsT=xw_c[:, ccols].bitcast(FP8X4), lhsT_scale=xs_c[:, ccols],
-                                    rhs=zw[:].bitcast(FP8X4), rhs_scale=zs[:], start=True, stop=True)
-                if hf == 1:
-                    if t == 0:
-                        nc.scalar.activation(out=s[:, t, cols], in_=dst, func=COPY, scale=0.0625)
-                    else:
-                        nc.vector.tensor_scalar(out=s[:, t, cols], in0=dst, scalar1=0.0625, scalar2=None, op0=ALU.mult)
-            if hf == 0:
-                nc.scalar.activation(out=s[:, :, cols], in_=acc0[:], func=COPY, scale=0.0625)
+            return zw, zs
+
+        def score(j, z, a, b):
+            zw, zs = z
+            ccols = slice(P * j, P * (j + 1))
+            nc.tensor.matmul_mx(out=s_acc[j][:, a:b], lhsT=xw_c[:, ccols].bitcast(FP8X4), lhsT_scale=xs_c[:, ccols],
+                                rhs=zw[:].bitcast(FP8X4), rhs_scale=zs[:], start=True, stop=True)
+            if a == 0 or j in (0, 3):
+                nc.scalar.activation(out=s[:, S * j + a : S * j + b], in_=s_acc[j][:, a:b], func=COPY, scale=0.0625)
+            else:
+                nc.vector.tensor_scalar(out=s[:, S * j + a : S * j + b], in0=s_acc[j][:, a:b], scalar1=0.0625, scalar2=None, op0=ALU.mult)
+
+        larger(*pieces[0])
+        for before, piece in zip(pieces[:-1], pieces[1:]):
+            larger(*piece)
+            less_h(*before)
+        zb_first = weigh(0, HALF)
+        less_h(*pieces[-1])
+        z_first = quantise(zb_first, 0)
+        z_last = quantise(weigh(HALF, S), HALF)
+        for pair in ((0, 1), (2, 3)):
+            for z, a, b in ((z_first, 0, HALF), (z_last, HALF, S)):
+                for j in pair:
+                    score(j, z, a, b)
 
         ow = tile([P, S], U32, "ow")
         osc = tile([P, S], U8, "osc")
         out_rows = out_0.rearrange("(p t) c -> p t c", t=4)
         out_words = out_1[0].rearrange("p n t -> p (n t)").bitcast(I32)
-        for hf in range(2):
-            cols = slice(HALF * hf, HALF * (hf + 1))
-            lcols = slice(8 * hf, 8 * hf + 8)
-            pa = tile([P, 4, HALF], F32, "pa_%d" % hf)
-            pb = tile([P, 4, HALF], F32, "pb_%d" % hf)
-            hi = tile([P, 4, HALF], F32, "hi_%d" % hf)
-            lo = tile([P, 4, HALF], F32, "lo_%d" % hf)
-            hi2 = tile([P, 4, HALF], F32, "hi2_%d" % hf)
-            lo2 = tile([P, 4, HALF], F32, "lo2_%d" % hf)
-            y = tile([P, 4, HALF], F32, "y_%d" % hf)
-            for t in range(4):
-                nc.scalar.activation(out=pa[:, t, :], in_=s[:, t, :].indirect(n3_t[:, lcols]), func=COPY)
-                nc.scalar.activation(out=pb[:, t, :], in_=s[:, t, :].indirect(n4_t[:, lcols]), func=COPY)
-            groups = [slice(0, 1), slice(1, 2), slice(2, 4)] if hf == 0 else [slice(0, 2), slice(2, 4)]
-            for ts in groups:
-                nc.vector.tensor_tensor(out=hi[:, ts, :], in0=pa[:, ts, :], in1=s[:, ts, cols], op=ALU.max)
-                nc.vector.tensor_tensor(out=lo[:, ts, :], in0=pa[:, ts, :], in1=s[:, ts, cols], op=ALU.min)
-                nc.vector.tensor_tensor(out=hi2[:, ts, :], in0=hi[:, ts, :], in1=pb[:, ts, :], op=ALU.max)
-                nc.vector.tensor_tensor(out=lo2[:, ts, :], in0=lo[:, ts, :], in1=pb[:, ts, :], op=ALU.min)
-                nc.vector.scalar_tensor_tensor(out=y[:, ts, :], in0=lo2[:, ts, :], scalar=-0.5, in1=hi2[:, ts, :], op0=ALU.mult, op1=ALU.add)
-                if ts.stop == 4 or hf == 1:
-                    st = ts if hf == 1 else slice(0, 4)
-                    nc.sync.dma_start(out=out_rows[:, st, cols], in_=y[:, st, :])
-            yb = tile([P, HALF, 4], BF16, "yb_%d" % hf)
-            yb_v = yb[:].rearrange("p (c i) t -> p c t i", i=4)
-            y_v = y[:].rearrange("p t (c i) -> p c t i", i=4)
-            if hf == 0:
-                nc.scalar.copy(out=yb_v, in_=y_v)
-            else:
-                nc.vector.tensor_copy(out=yb_v, in_=y_v)
-            nc.vector.quantize_mx(out=ow[:, cols].bitcast(FP8X4), scales=osc[:, cols], in_=yb[:].rearrange("p c t -> p (c t)"))
-            nc.scalar.dma_start(out=out_words[:, cols], in_=ow[:, cols].bitcast(I32))
+        pa = tile([P, 4, S], F32, "pa")
+        pb = tile([P, 4, S], F32, "pb")
+        hi = tile([P, 4, S], F32, "hi")
+        lo = tile([P, 4, S], F32, "lo")
+        hi2 = tile([P, 4, S], F32, "hi2")
+        lo2 = tile([P, 4, S], F32, "lo2")
+        y = tile([P, 4, S], F32, "y")
+        halves = [(0, HALF), (HALF, S)]
+        for t in range(4):
+            spans = halves if t == 3 else [(0, S)]
+            for a, b in spans:
+                fetch(False, pa, s, n3_t, t, a, b, scale=-0.5)
+            for a, b in spans:
+                fetch(t in (0,), pb, s, n4_t, t, a, b)
+            nc.vector.scalar_tensor_tensor(out=hi[:, t, :], in0=pa[:, t, :], scalar=-32.0, in1=s_acc[t][:], op0=ALU.mult, op1=ALU.max)
+            nc.vector.scalar_tensor_tensor(out=lo[:, t, :], in0=s_acc[t][:], scalar=-0.03125, in1=pa[:, t, :], op0=ALU.mult, op1=ALU.max)
+            for a, b in spans:
+                nc.vector.scalar_tensor_tensor(out=hi2[:, t, a:b], in0=hi[:, t, a:b], scalar=0.0625, in1=pb[:, t, a:b], op0=ALU.mult, op1=ALU.max)
+                nc.vector.scalar_tensor_tensor(out=lo2[:, t, a:b], in0=pb[:, t, a:b], scalar=-0.5, in1=lo[:, t, a:b], op0=ALU.mult, op1=ALU.max)
+            adder = nc.gpsimd if t < 3 else nc.vector
+            for a, b in spans:
+                adder.tensor_tensor(out=y[:, t, a:b], in0=hi2[:, t, a:b], in1=lo2[:, t, a:b], op=ALU.add)
+            nc.sync.dma_start(out=out_rows[:, t, :], in_=y[:, t, :])
+        yb = [tile([P, HALF, 4], BF16, "yb_%d" % a) for a, b in halves]
+        for (a, b), dst, mover in zip(halves, yb, (nc.scalar.copy, nc.vector.tensor_copy)):
+            mover(out=dst[:].rearrange("p (c i) t -> p c t i", i=4), in_=y[:, :, a:b].rearrange("p t (c i) -> p c t i", i=4))
+        for (a, b), src in zip(halves, yb):
+            nc.vector.quantize_mx(out=ow[:, a:b].bitcast(FP8X4), scales=osc[:, a:b], in_=src[:].rearrange("p c t -> p (c t)"))
+        nc.sync.dma_start(out=out_words, in_=ow[:].bitcast(I32))
         for q in range(4):
-            eng = nc.sync if q % 2 == 0 else nc.scalar
+            eng = nc.scalar if q % 2 == 0 else nc.sync
             eng.dma_start(out=out_2[0, 4 * q : 4 * q + 4, :].bitcast(I32), in_=osc[32 * q : 32 * q + 4, :].bitcast(I32))

@@ -157,17 +157,16 @@ def tile_picked_pqcoverrange_none_po_kernel(tc, x_words, x_scales, d_words, d_sc
         for t in range(4):
             spans = halves if t == 3 else [(0, S)]
             for a, b in spans:
-                fetch(False, pa, s, n3_t, t, a, b, scale=-0.5)
+                fetch(False, pa, s, n3_t, t, a, b)
             for a, b in spans:
-                fetch(t in (0,), pb, s, n4_t, t, a, b)
-            nc.vector.scalar_tensor_tensor(out=hi[:, t, :], in0=pa[:, t, :], scalar=-32.0, in1=s_acc[t][:], op0=ALU.mult, op1=ALU.max)
-            nc.vector.scalar_tensor_tensor(out=lo[:, t, :], in0=s_acc[t][:], scalar=-0.03125, in1=pa[:, t, :], op0=ALU.mult, op1=ALU.max)
+                fetch(t in (), pb, s, n4_t, t, a, b)
+            nc.vector.tensor_tensor(out=hi[:, t, :], in0=pa[:, t, :], in1=s[:, S * t : S * (t + 1)], op=ALU.max)
+            nc.vector.tensor_tensor(out=lo[:, t, :], in0=pa[:, t, :], in1=s[:, S * t : S * (t + 1)], op=ALU.min)
             for a, b in spans:
-                nc.vector.scalar_tensor_tensor(out=hi2[:, t, a:b], in0=hi[:, t, a:b], scalar=0.0625, in1=pb[:, t, a:b], op0=ALU.mult, op1=ALU.max)
-                nc.vector.scalar_tensor_tensor(out=lo2[:, t, a:b], in0=pb[:, t, a:b], scalar=-0.5, in1=lo[:, t, a:b], op0=ALU.mult, op1=ALU.max)
-            adder = nc.gpsimd if t < 3 else nc.vector
+                nc.vector.tensor_tensor(out=hi2[:, t, a:b], in0=hi[:, t, a:b], in1=pb[:, t, a:b], op=ALU.max)
+                nc.vector.tensor_tensor(out=lo2[:, t, a:b], in0=lo[:, t, a:b], in1=pb[:, t, a:b], op=ALU.min)
             for a, b in spans:
-                adder.tensor_tensor(out=y[:, t, a:b], in0=hi2[:, t, a:b], in1=lo2[:, t, a:b], op=ALU.add)
+                nc.vector.scalar_tensor_tensor(out=y[:, t, a:b], in0=lo2[:, t, a:b], scalar=-0.5, in1=hi2[:, t, a:b], op0=ALU.mult, op1=ALU.add)
             nc.sync.dma_start(out=out_rows[:, t, :], in_=y[:, t, :])
         yb = [tile([P, HALF, 4], BF16, "yb_%d" % a) for a, b in halves]
         for (a, b), dst, mover in zip(halves, yb, (nc.scalar.copy, nc.vector.tensor_copy)):

@@ -56,7 +56,7 @@ def tile_picked_pqcoverrange_none_po_kernel(tc, x_words, x_scales, d_words, d_sc
         ds_g = late.tile([P, H], U8, name="ds_g", align_bytes=64, offset=4096)
         nc.vector.tensor_copy(out=ds_g[:], in_=ds_tab[:].indirect(k1_t[:]))
         ds_mm = tile([P, H], U8, "ds_mm")
-        nc.vector.tensor_copy(out=ds_mm[:].rearrange("p (t m) -> p m t", t=4), in_=ds_g[:].rearrange("p (m t) -> p m t", t=4))
+        nc.vector.tensor_copy(out=ds_mm[:].rearrange("p (t m) -> p t m", t=4), in_=ds_g[:].rearrange("p (m t) -> p t m", t=4))
         for e in range(2):
             nc.scalar.dma_start(out=ds_mm[2 + e : P : 32, :].bitcast(I32), in_=ds_mm[16 + e : P : 32, :].bitcast(I32))
         xs_o = late.tile([P, S], U8, name="xs_o", offset=4096, align_bytes=64)
@@ -79,9 +79,11 @@ def tile_picked_pqcoverrange_none_po_kernel(tc, x_words, x_scales, d_words, d_sc
             nc.scalar.activation(out=h[:, S * t : S * (t + 1)], in_=acc[:], func=COPY, scale=0.0625)
 
         xw_c = late.tile([P, C], U32, name="xw_c", offset=64 + C + 4 * S, align_bytes=64)
-        xs_c = late.tile([P, C], U8, name="xs_c", offset=64, align_bytes=64)
-        nc.vector.tensor_copy(out=xs_c[:].rearrange("p (t m) -> p m t", t=4), in_=xs_tab[:].indirect(cand_t[:]))
+        xs_g = late.tile([P, C], U8, name="xs_g", offset=64, align_bytes=64)
+        nc.vector.tensor_copy(out=xs_g[:], in_=xs_tab[:].indirect(cand_t[:]))
         nc.vector.tensor_copy(out=xw_c[:].rearrange("p (t m) -> p m t", t=4), in_=xw_tab[:].indirect(cand_t[:]))
+        xs_c = tile([P, C], U8, "xs_c")
+        nc.vector.tensor_copy(out=xs_c[:].rearrange("p (t m) -> p t m", t=4), in_=xs_g[:].rearrange("p (m t) -> p t m", t=4))
 
         pieces = [(0, 0, S), (1, 0, S), (2, 0, S), (3, 0, HALF), (3, HALF, S)]
 
@@ -97,6 +99,7 @@ def tile_picked_pqcoverrange_none_po_kernel(tc, x_words, x_scales, d_words, d_sc
         g2 = tile([P, 4, S], F32, "g2")
         mx = tile([P, 4, S], F32, "mx")
         u = tile([P, 4, S], F32, "u")
+        z = tile([P, 4, S], F32, "z")
         s = tile([P, 4 * S], F32, "s")
         s_acc = [ps.tile([P, S], F32, name="s_acc", tag="s%d" % t) for t in range(4)]
         def larger(t, a, b):
@@ -107,40 +110,33 @@ def tile_picked_pqcoverrange_none_po_kernel(tc, x_words, x_scales, d_words, d_sc
         def less_h(t, a, b):
             nc.vector.scalar_tensor_tensor(out=u[:, t, a:b], in0=h[:, S * t + a : S * t + b], scalar=-0.75, in1=mx[:, t, a:b], op0=ALU.mult, op1=ALU.add)
 
-        def weigh(a, b):
+        def weigh(t, a, b):
+            nc.vector.tensor_scalar(out=z[:, t, a:b], in0=u[:, t, a:b], scalar1=gs_t[:, t : t + 1], scalar2=None, op0=ALU.mult)
+
+        def weave(mover, a, b):
             zb = tile([P, HALF, 4], BF16, "zb_%d" % a)
-            nc.vector.tensor_tensor(out=zb[:].rearrange("p (c i) t -> p c t i", i=4), in0=u[:, :, a:b].rearrange("p t (c i) -> p c t i", i=4),
-                                    in1=gs_t[:].unsqueeze(1).unsqueeze(3).to_broadcast([P, HALF // 4, 4, 4]), op=ALU.mult)
+            mover(out=zb[:].rearrange("p (c i) t -> p c t i", i=4), in_=z[:, :, a:b].rearrange("p t (c i) -> p c t i", i=4))
             return zb
 
-        def quantise(zb, a):
-            zw = tile([P, HALF], U32, "zw_%d" % a)
-            zs = tile([P, HALF], U8, "zs_%d" % a)
-            nc.vector.quantize_mx(out=zw[:].bitcast(FP8X4), scales=zs[:], in_=zb[:].rearrange("p c t -> p (c t)"))
-            return zw, zs
-
-        def score(j, z, a, b):
-            zw, zs = z
+        steps = (larger, less_h, weigh)
+        for turn in range(len(pieces) + len(steps) - 1):
+            for lag, step in enumerate(steps):
+                if 0 <= turn - lag < len(pieces):
+                    step(*pieces[turn - lag])
+        zb_first = weave(nc.scalar.copy, 0, HALF)
+        zb_last = weave(nc.vector.tensor_copy, HALF, S)
+        zw = tile([P, S], U32, "zw")
+        zs = tile([P, S], U8, "zs")
+        for zb, a, b in ((zb_first, 0, HALF), (zb_last, HALF, S)):
+            nc.vector.quantize_mx(out=zw[:, a:b].bitcast(FP8X4), scales=zs[:, a:b], in_=zb[:].rearrange("p c t -> p (c t)"))
+        for j in range(4):
             ccols = slice(P * j, P * (j + 1))
-            nc.tensor.matmul_mx(out=s_acc[j][:, a:b], lhsT=xw_c[:, ccols].bitcast(FP8X4), lhsT_scale=xs_c[:, ccols],
+            nc.tensor.matmul_mx(out=s_acc[j][:], lhsT=xw_c[:, ccols].bitcast(FP8X4), lhsT_scale=xs_c[:, ccols],
                                 rhs=zw[:].bitcast(FP8X4), rhs_scale=zs[:], start=True, stop=True)
-            if a == 0 or j in (0, 3):
-                nc.scalar.activation(out=s[:, S * j + a : S * j + b], in_=s_acc[j][:, a:b], func=COPY, scale=0.0625)
+            if j in (0,):
+                nc.scalar.activation(out=s[:, S * j : S * (j + 1)], in_=s_acc[j][:], func=COPY, scale=0.0625)
             else:
-                nc.vector.tensor_scalar(out=s[:, S * j + a : S * j + b], in0=s_acc[j][:, a:b], scalar1=0.0625, scalar2=None, op0=ALU.mult)
-
-        larger(*pieces[0])
-        for before, piece in zip(pieces[:-1], pieces[1:]):
-            larger(*piece)
-            less_h(*before)
-        zb_first = weigh(0, HALF)
-        less_h(*pieces[-1])
-        z_first = quantise(zb_first, 0)
-        z_last = quantise(weigh(HALF, S), HALF)
-        for pair in ((0, 1), (2, 3)):
-            for z, a, b in ((z_first, 0, HALF), (z_last, HALF, S)):
-                for j in pair:
-                    score(j, z, a, b)
+                nc.vector.tensor_scalar(out=s[:, S * j : S * (j + 1)], in0=s_acc[j][:], scalar1=0.0625, scalar2=None, op0=ALU.mult)
 
         ow = tile([P, S], U32, "ow")
         osc = tile([P, S], U8, "osc")

from contextlib import ExitStack

import concourse.mybir as mybir

F32 = mybir.dt.float32
BF16 = mybir.dt.bfloat16
I32 = mybir.dt.int32
U32 = mybir.dt.uint32
U16 = mybir.dt.uint16
U8 = mybir.dt.uint8
FP8X4 = mybir.dt.float8_e4m3fn_x4
ALU = mybir.AluOpType
COPY = mybir.ActivationFunctionType.Copy

P = 128
K, T, S, G, H, C = 512, 1024, 256, 2048, 512, 512
HALF = S // 2
FLOPS = 2 * K * H * S + 2 * K * C * S


def tile_picked_pqcoverrange_none_po_kernel(tc, x_words, x_scales, d_words, d_scales, gs, offs, k1, n1, n2, cand, n3, n4, out_0, out_1, out_2):
    nc = tc.nc
    with ExitStack() as ctx:
        sb = ctx.enter_context(tc.tile_pool(name="sb", bufs=1))
        late = ctx.enter_context(tc.tile_pool(name="late", bufs=1))
        ps = ctx.enter_context(tc.psum_pool(name="ps", bufs=1))

        def tile(shape, dtype, name):
            return sb.tile(shape, dtype, name=name, align_bytes=64)

        def load_list(src, name):
            t = tile(list(src.shape), U16, name)
            nc.sync.dma_start(out=t[:], in_=src)
            return t

        ds_tab = tile([P, G], U8, "ds_tab")
        xs_tab = tile([P, T], U8, "xs_tab")
        nc.gpsimd.memset(xs_tab[:].bitcast(U32), 0)
        k1_t = load_list(k1, "k1_t")
        ds_rows = d_scales[0].bitcast(I32)
        for e in range(2):
            nc.sync.dma_start(out=ds_tab[e:P:2, :].bitcast(I32), in_=ds_rows[e:16:2, :].unsqueeze(1).to_broadcast([8, 8, G // 4]))
        dw_tab = tile([P, G], U32, "dw_tab")
        nc.sync.dma_start(out=dw_tab[:].bitcast(I32), in_=d_words[0].rearrange("p n t -> p (n t)").bitcast(I32))
        for q in range(4):
            nc.scalar.dma_start(out=xs_tab[32 * q : 32 * q + 4, :].bitcast(I32), in_=x_scales[0, 4 * q : 4 * q + 4, :].bitcast(I32))
        offs_t = load_list(offs, "offs_t")
        xw_tab = tile([P, T], U32, "xw_tab")
        nc.sync.dma_start(out=xw_tab[:].bitcast(I32), in_=x_words[0].rearrange("p n t -> p (n t)").bitcast(I32))
        cand_t = load_list(cand, "cand_t")
        n1_t = load_list(n1, "n1_t")
        n2_t = load_list(n2, "n2_t")
        n3_t = load_list(n3, "n3_t")
        n4_t = load_list(n4, "n4_t")

        ds_g = late.tile([P, H], U8, name="ds_g", align_bytes=64, offset=4096)
        nc.vector.tensor_copy(out=ds_g[:], in_=ds_tab[:].indirect(k1_t[:]))
        ds_mm = tile([P, H], U8, "ds_mm")
        nc.vector.tensor_copy(out=ds_mm[:].rearrange("p (t m) -> p t m", t=4), in_=ds_g[:].rearrange("p (m t) -> p t m", t=4))
        for e in range(2):
            nc.scalar.dma_start(out=ds_mm[2 + e : P : 32, :].bitcast(I32), in_=ds_mm[16 + e : P : 32, :].bitcast(I32))
        xs_o = late.tile([P, S], U8, name="xs_o", offset=4096, align_bytes=64)
        nc.vector.tensor_copy(out=xs_o[:], in_=xs_tab[:].indirect(offs_t[:]))
        dw_g = late.tile([P, H], U32, name="dw_g", offset=0, align_bytes=64)
        nc.vector.tensor_copy(out=dw_g[:], in_=dw_tab[:].indirect(k1_t[:]))
        dw_d = tile([P, H], U32, "dw_d")
        nc.vector.tensor_copy(out=dw_d[:].rearrange("p (t m) -> p m t", t=4), in_=dw_g[:].rearrange("p (m t) -> p m t", t=4))
        xw_o = late.tile([P, S], U32, name="xw_o", offset=64 + C, align_bytes=64)
        nc.vector.tensor_copy(out=xw_o[:], in_=xw_tab[:].indirect(offs_t[:]))
        gs_t = late.tile([P, 4], F32, name="gs_t", align_bytes=64, offset=0)
        nc.sync.dma_start(out=gs_t[:], in_=gs.rearrange("(p t) o -> p (t o)", t=4))

        h = tile([P, 4 * S], F32, "h")
        for t in range(4):
            acc = ps.tile([P, S], F32, name="acc", tag="h%d" % t)
            cols = slice(P * t, P * (t + 1))
            nc.tensor.matmul_mx(out=acc[:], lhsT=dw_d[:, cols].bitcast(FP8X4), lhsT_scale=ds_mm[:, cols],
                                rhs=xw_o[:].bitcast(FP8X4), rhs_scale=xs_o[:], start=True, stop=True)
            nc.scalar.activation(out=h[:, S * t : S * (t + 1)], in_=acc[:], func=COPY, scale=0.0625)

        xw_c = late.tile([P, C], U32, name="xw_c", offset=64 + C + 4 * S, align_bytes=64)
        xs_g = late.tile([P, C], U8, name="xs_g", offset=64, align_bytes=64)
        nc.vector.tensor_copy(out=xs_g[:], in_=xs_tab[:].indirect(cand_t[:]))
        nc.vector.tensor_copy(out=xw_c[:].rearrange("p (t m) -> p m t", t=4), in_=xw_tab[:].indirect(cand_t[:]))
        xs_c = tile([P, C], U8, "xs_c")
        nc.vector.tensor_copy(out=xs_c[:].rearrange("p (t m) -> p t m", t=4), in_=xs_g[:].rearrange("p (m t) -> p t m", t=4))

        pieces = [(0, 0, S), (1, 0, S), (2, 0, S), (3, 0, HALF), (3, HALF, S)]

        def fetch(on_vector, dst, src, lst, t, a, b, scale=1.0):
            width = 2 * S if b - a == S else S
            window = src[:, S * t : S * t + width].indirect(lst[:, a // 16 : b // 16])
            if on_vector:
                nc.vector.tensor_copy(out=dst[:, t, a:b], in_=window)
            else:
                nc.scalar.activation(out=dst[:, t, a:b], in_=window, func=COPY, scale=scale)

        g1 = tile([P, 4, S], F32, "g1")
        g2 = tile([P, 4, S], F32, "g2")
        mx = tile([P, 4, S], F32, "mx")
        u = tile([P, 4, S], F32, "u")
        z = tile([P, 4, S], F32, "z")
        s = tile([P, 4 * S], F32, "s")
        s_acc = [ps.tile([P, S], F32, name="s_acc", tag="s%d" % t) for t in range(4)]
        def larger(t, a, b):
            fetch(False, g1, h, n1_t, t, a, b)
            fetch(t in (0, 1), g2, h, n2_t, t, a, b)
            nc.vector.tensor_tensor(out=mx[:, t, a:b], in0=g1[:, t, a:b], in1=g2[:, t, a:b], op=ALU.max)

        def less_h(t, a, b):
            nc.vector.scalar_tensor_tensor(out=u[:, t, a:b], in0=h[:, S * t + a : S * t + b], scalar=-0.75, in1=mx[:, t, a:b], op0=ALU.mult, op1=ALU.add)

        def weigh(t, a, b):
            nc.vector.tensor_scalar(out=z[:, t, a:b], in0=u[:, t, a:b], scalar1=gs_t[:, t : t + 1], scalar2=None, op0=ALU.mult)

        def weave(mover, a, b):
            zb = tile([P, HALF, 4], BF16, "zb_%d" % a)
            mover(out=zb[:].rearrange("p (c i) t -> p c t i", i=4), in_=z[:, :, a:b].rearrange("p t (c i) -> p c t i", i=4))
            return zb

        steps = (larger, less_h, weigh)
        for turn in range(len(pieces) + len(steps) - 1):
            for lag, step in enumerate(steps):
                if 0 <= turn - lag < len(pieces):
                    step(*pieces[turn - lag])
        zb_first = weave(nc.scalar.copy, 0, HALF)
        zb_last = weave(nc.vector.tensor_copy, HALF, S)
        zw = tile([P, S], U32, "zw")
        zs = tile([P, S], U8, "zs")
        for zb, a, b in ((zb_first, 0, HALF), (zb_last, HALF, S)):
            nc.vector.quantize_mx(out=zw[:, a:b].bitcast(FP8X4), scales=zs[:, a:b], in_=zb[:].rearrange("p c t -> p (c t)"))
        for j in range(4):
            ccols = slice(P * j, P * (j + 1))
            nc.tensor.matmul_mx(out=s_acc[j][:], lhsT=xw_c[:, ccols].bitcast(FP8X4), lhsT_scale=xs_c[:, ccols],
                                rhs=zw[:].bitcast(FP8X4), rhs_scale=zs[:], start=True, stop=True)
            if j in (0,):
                nc.scalar.activation(out=s[:, S * j : S * (j + 1)], in_=s_acc[j][:], func=COPY, scale=0.0625)
            else:
                nc.vector.tensor_scalar(out=s[:, S * j : S * (j + 1)], in0=s_acc[j][:], scalar1=0.0625, scalar2=None, op0=ALU.mult)

        ow = tile([P, S], U32, "ow")
        osc = tile([P, S], U8, "osc")
        out_rows = out_0.rearrange("(p t) c -> p t c", t=4)
        out_words = out_1[0].rearrange("p n t -> p (n t)").bitcast(I32)
        pa = tile([P, 4, S], F32, "pa")
        pb = tile([P, 4, S], F32, "pb")
        hi = tile([P, 4, S], F32, "hi")
        lo = tile([P, 4, S], F32, "lo")
        hi2 = tile([P, 4, S], F32, "hi2")
        lo2 = tile([P, 4, S], F32, "lo2")
        y = tile([P, 4, S], F32, "y")
        halves = [(0, HALF), (HALF, S)]
        for t in range(4):
            spans = halves if t == 3 else [(0, S)]
            for a, b in spans:
                fetch(False, pa, s, n3_t, t, a, b)
            for a, b in spans:
                fetch(t in (), pb, s, n4_t, t, a, b)
            nc.vector.tensor_tensor(out=hi[:, t, :], in0=pa[:, t, :], in1=s[:, S * t : S * (t + 1)], op=ALU.max)
            nc.vector.tensor_tensor(out=lo[:, t, :], in0=pa[:, t, :], in1=s[:, S * t : S * (t + 1)], op=ALU.min)
            for a, b in spans:
                nc.vector.tensor_tensor(out=hi2[:, t, a:b], in0=hi[:, t, a:b], in1=pb[:, t, a:b], op=ALU.max)
                nc.vector.tensor_tensor(out=lo2[:, t, a:b], in0=lo[:, t, a:b], in1=pb[:, t, a:b], op=ALU.min)
            for a, b in spans:
                nc.vector.scalar_tensor_tensor(out=y[:, t, a:b], in0=lo2[:, t, a:b], scalar=-0.5, in1=hi2[:, t, a:b], op0=ALU.mult, op1=ALU.add)
            nc.sync.dma_start(out=out_rows[:, t, :], in_=y[:, t, :])
        yb = [tile([P, HALF, 4], BF16, "yb_%d" % a) for a, b in halves]
        for (a, b), dst, mover in zip(halves, yb, (nc.scalar.copy, nc.vector.tensor_copy)):
            mover(out=dst[:].rearrange("p (c i) t -> p c t i", i=4), in_=y[:, :, a:b].rearrange("p t (c i) -> p c t i", i=4))
        for (a, b), src in zip(halves, yb):
            nc.vector.quantize_mx(out=ow[:, a:b].bitcast(FP8X4), scales=osc[:, a:b], in_=src[:].rearrange("p c t -> p (c t)"))
        nc.sync.dma_start(out=out_words, in_=ow[:].bitcast(I32))
        for q in range(4):
            eng = nc.scalar if q % 2 == 0 else nc.sync
            eng.dma_start(out=out_2[0, 4 * q : 4 * q + 4, :].bitcast(I32), in_=osc[32 * q : 32 * q + 4, :].bitcast(I32))
